import numpy as np
import ml_dtypes


def mxq(x, axis, fmt="e4m3"):
    dtype, down = {"e4m3": (ml_dtypes.float8_e4m3fn, 7), "e5m2": (ml_dtypes.float8_e5m2, 14)}[fmt]
    v = np.moveaxis(np.asarray(x, np.float32).astype(ml_dtypes.bfloat16).astype(np.float64), axis, -1)
    blocks = v.reshape(v.shape[:-1] + (-1, 32))
    amax = np.abs(blocks).max(-1, keepdims=True)
    byte = np.maximum(np.where(amax > 0, np.frexp(amax)[1] - 1 + 127, 0) - down, 1)
    scale = np.exp2(byte - 127.0)
    codes = (blocks / scale).astype(np.float32).astype(dtype).astype(np.float64)
    return np.moveaxis((codes * scale).reshape(v.shape), -1, axis)


WIDE = False


def mx_kscale(k):
    if not WIDE:
        return np.ones(k)
    levels = np.array([10, -10, 5, -5, 0])
    if k % 512:
        return np.exp2(np.random.permutation(np.resize(levels, k // 32))).repeat(32)
    a = np.empty((k // 512, 16))
    for p in range(k // 512):
        a[p, :8] = np.random.permutation(np.resize(levels, 8))
        for g in range(8):
            far = levels[np.abs(levels - a[p, g]) >= 10]
            a[p, g + 8] = far[np.random.randint(len(far))]
    return np.exp2(a.ravel()).repeat(32)


def f64(x):
    return np.asarray(x).astype(np.float64)


def striped(idx):
    return np.tile(idx.reshape(-1, 16).T, (8, 1)).astype(np.uint16)


def unstriped(offs):
    return offs[:16].T.reshape(-1).astype(np.int64)


def pack_weight(w):
    k, n = w.shape
    w = f64(np.asarray(w, np.float32).astype(ml_dtypes.bfloat16)).reshape(k // 32, 32, n)
    amax = np.abs(w).max(1)
    byte = np.clip(np.where(amax > 0, np.frexp(amax)[1] - 1 + 127 - 7, 1), 1, 254)
    scaled = (w * np.exp2(127.0 - byte)[:, None, :]).reshape(k, n).astype(np.float32)
    words = np.ascontiguousarray(scaled.reshape(k // 512, 128, 4, n).transpose(0, 1, 3, 2)).astype(ml_dtypes.float8_e4m3fn).view(np.uint8)
    return words, np.ascontiguousarray(byte.astype(np.uint8).reshape(k // 512, 16, n))


def unpack_weight(words, scales):
    g, p, n, _ = words.shape
    vals = np.ascontiguousarray(words).view(ml_dtypes.float8_e4m3fn).astype(np.float64) * np.repeat(np.exp2(scales.astype(np.float64) - 127.0), 8, axis=1)[..., None]
    return vals.transpose(0, 1, 3, 2).reshape(g * 512, n)


def relu(v):
    return np.maximum(v, 0.0)

def planes(y):
    n, m = y.shape
    v = y.astype(np.float32).astype(ml_dtypes.bfloat16).astype(np.float64).reshape(n // 32, 32, m)
    top = np.abs(v).max(1)
    byte = np.clip(np.where(top > 0, np.frexp(top)[1] - 1 + 127 - 7, 1), 1, 254)
    codes = (v * np.exp2(127.0 - byte)[:, None, :]).reshape(n, m).astype(np.float32).astype(ml_dtypes.float8_e4m3fn).view(np.uint8)
    words = codes.reshape(n // 512, 128, 4, m).transpose(0, 1, 3, 2)
    return np.ascontiguousarray(words), np.ascontiguousarray(byte.astype(np.uint8).reshape(n // 512, 16, m))


K, T, S, V, H = 512, 2048, 512, 512, 512


def setup_inputs():
    n = np.random.standard_normal
    s = mx_kscale(K)[:, None]
    packed_xT = pack_weight(n((K, T)) * s)
    packed_w1 = pack_weight(n((K, H)) / np.sqrt(K) / s)
    return {
        "x_words": packed_xT[0],
        "x_scales": packed_xT[1],
        "w1_words": packed_w1[0],
        "w1_scales": packed_w1[1],
        "gs": (np.random.uniform(0.5, 1.5, (K, 1)) / s).astype(np.float32),
        "offs": striped(np.random.permutation(T)[:S]),
        "ca": striped(np.random.permutation(T)[:V]),
        "cb": striped(np.random.permutation(T)[:V]),
    }


def reference(x_words, x_scales, w1_words, w1_scales, gs, offs, ca, cb):
    x_ca = unpack_weight(x_words, x_scales)[:, unstriped(ca)]
    xq = unpack_weight(x_words, x_scales)[:, unstriped(offs)]
    h = relu(unpack_weight(w1_words, w1_scales).T @ xq)
    z = f64(gs) * h
    zq = mxq(z, 0, "e4m3")
    a = 0.0625 * (x_ca.T @ zq)
    x_cb = unpack_weight(x_words, x_scales)[:, unstriped(cb)]
    b = 0.0625 * (x_cb.T @ zq)
    out_0 = np.tanh(a - b)
    return (out_0,) + planes(out_0)

@@ -1,0 +1,161 @@
+from contextlib import ExitStack
+
+import concourse.mybir as mybir
+
+FLOPS = 805306368
+
+F32 = mybir.dt.float32
+BF16 = mybir.dt.bfloat16
+I32 = mybir.dt.int32
+U32 = mybir.dt.uint32
+U16 = mybir.dt.uint16
+U8 = mybir.dt.uint8
+FP8X4 = mybir.dt.float8_e4m3fn_x4
+ALU = mybir.AluOpType
+ACT = mybir.ActivationFunctionType
+
+P = 128
+PACK = 4
+T = 2048
+S = 512
+CH = 128
+NCH = S // CH
+
+
+def tile_picked_candtwo_tanh_po_kernel(
+    tc, x_words, x_scales, w1_words, w1_scales, gs, offs, ca, cb, out_0, out_1, out_2
+):
+    nc = tc.nc
+    with ExitStack() as ctx:
+        keep = ctx.enter_context(tc.tile_pool(name="keep", bufs=1))
+        psum = ctx.enter_context(tc.psum_pool(name="psum", bufs=1))
+
+        def sb(shape, dtype, name, tag=None):
+            return keep.tile(shape, dtype, name=name, tag=tag or name, align_bytes=64)
+
+        offs_t = keep.tile([P, S // 16], U16, name="offs_t")
+        ca_t = keep.tile([P, S // 16], U16, name="ca_t")
+        cb_t = keep.tile([P, S // 16], U16, name="cb_t")
+        xw = sb([P, T], I32, "xw")
+        xs = sb([P, T], U8, "xs")
+        ww = sb([P, S], I32, "ww")
+        ws = sb([P, S], U8, "ws", "slot_b")
+        gain = sb([P, PACK], F32, "gain")
+
+        def spread(rows, width):
+            return rows.bitcast(I32).unsqueeze(0).to_broadcast([8, 4, width // 4])
+
+        nc.sync.dma_start(offs_t[:], offs)
+        for q in range(4):
+            nc.sync.dma_start(xs[32 * q : 32 * q + 32, :].bitcast(I32), spread(x_scales[0, 4 * q : 4 * q + 4, :], T))
+        nc.sync.dma_start(ca_t[:], ca)
+        nc.sync.dma_start(cb_t[:], cb)
+        nc.sync.dma_start(xw[:], x_words[0].rearrange("p n t -> p (n t)").bitcast(I32))
+        nc.sync.dma_start(ww[:], w1_words[0].rearrange("p n t -> p (n t)").bitcast(I32))
+        for q in range(4):
+            nc.sync.dma_start(ws[32 * q : 32 * q + 32, :].bitcast(I32), spread(w1_scales[0, 4 * q : 4 * q + 4, :], S))
+        nc.sync.dma_start(gain[:], gs.rearrange("(p t) o -> p (t o)", t=PACK))
+
+        tok_w = sb([P, S], U32, "tok_w")
+        tok_s = sb([P, S], U8, "tok_s")
+        pair_s_raw = sb([P, 2, S], U8, "pair_s_raw")
+        pair_s = sb([P, 2, S], U8, "pair_s")
+        wd_w = sb([P, S], I32, "wd_w")
+        wd_s = sb([P, S], U8, "wd_s")
+
+        nc.vector.tensor_copy(tok_s[:], xs[:].indirect(offs_t[:]))
+        nc.vector.tensor_copy(pair_s_raw[:, 0, :], xs[:].indirect(ca_t[:]))
+        nc.vector.tensor_copy(pair_s_raw[:, 1, :], xs[:].indirect(cb_t[:]))
+        nc.vector.tensor_copy(tok_w[:], xw[:].bitcast(U32).indirect(offs_t[:]))
+        nc.vector.tensor_copy(
+            wd_w[:].rearrange("p (t m) -> p m t", t=PACK), ww[:].rearrange("p (m t) -> p m t", t=PACK)
+        )
+        nc.vector.tensor_copy(
+            wd_s[:].rearrange("p (t m) -> p t m", t=PACK), ws[:].rearrange("p (m t) -> p t m", t=PACK)
+        )
+        nc.vector.tensor_copy(
+            pair_s[:].rearrange("p l (t m) -> p l t m", t=PACK),
+            pair_s_raw[:].rearrange("p l (m t) -> p l t m", t=PACK),
+        )
+        pair_w = []
+        for lst, slot in ((ca_t, "slot_a"), (cb_t, "slot_b")):
+            picked = sb([P, S], U32, "picked_" + slot, slot)
+            nc.vector.tensor_copy(picked[:].rearrange("p (t m) -> p m t", t=PACK), xw[:].bitcast(U32).indirect(lst[:]))
+            pair_w.append(picked)
+
+        hid = []
+        for c in range(NCH):
+            cols = slice(c * CH, (c + 1) * CH)
+            bank = psum.tile([P, PACK, CH], F32, name="hid%d" % c)
+            for t in range(PACK):
+                m = slice(t * P, (t + 1) * P)
+                nc.tensor.matmul_mx(
+                    out=bank[:, t, :],
+                    lhsT=wd_w[:, m].bitcast(FP8X4),
+                    lhsT_scale=wd_s[:, m],
+                    rhs=tok_w[:, cols].bitcast(FP8X4),
+                    rhs_scale=tok_s[:, cols],
+                    start=True,
+                    stop=True,
+                )
+            hid.append(bank)
+
+        diffs = []
+        for c in range(NCH):
+            z = sb([P, 2, CH * PACK], BF16, "z%d" % c)
+            z_w = sb([P, 2, CH], U32, "z_w%d" % c)
+            z_s = sb([P, 2, CH], U8, "z_s%d" % c)
+            nc.vector.scalar_tensor_tensor(
+                out=z[:, 0, :].rearrange("p (n t) -> p n t", t=PACK),
+                in0=hid[c][:].rearrange("p t n -> p n t"),
+                scalar=0.0,
+                in1=gain[:].unsqueeze(1).to_broadcast([P, CH, PACK]),
+                op0=ALU.max,
+                op1=ALU.mult,
+            )
+            nc.vector.tensor_scalar(out=z[:, 1, :], in0=z[:, 0, :], scalar1=-1.0, scalar2=None, op0=ALU.mult)
+            nc.vector.quantize_mx(
+                out=z_w[:].rearrange("p l n -> p (l n)").bitcast(FP8X4),
+                scales=z_s[:].rearrange("p l n -> p (l n)"),
+                in_=z[:].rearrange("p l n -> p (l n)"),
+            )
+            diff = psum.tile([P, PACK, CH], F32, name="diff%d" % c)
+            for t in range(PACK):
+                m = slice(t * P, (t + 1) * P)
+                for l in range(2):
+                    nc.tensor.matmul_mx(
+                        out=diff[:, t, :],
+                        lhsT=pair_w[l][:, m].bitcast(FP8X4),
+                        lhsT_scale=pair_s[:, l, m],
+                        rhs=z_w[:, l, :].bitcast(FP8X4),
+                        rhs_scale=z_s[:, l, :],
+                        start=(l == 0),
+                        stop=(l == 1),
+                    )
+            diffs.append(diff)
+
+        out_w = sb([P, S], U32, "out_w")
+        out_s = sb([P, S], U8, "out_s")
+        rows = out_0.rearrange("(p t) n -> p t n", t=PACK)
+        words_out = out_1[0].rearrange("p n t -> p (n t)").bitcast(I32)
+        for c in range(NCH):
+            cols = slice(c * CH, (c + 1) * CH)
+            diff = diffs[c]
+            y16 = sb([P, CH, PACK], BF16, "y16_%d" % c)
+            y32 = sb([P, PACK, CH], F32, "y32_%d" % c)
+            if c != 2:
+                nc.scalar.activation(y16[:], diff[:].rearrange("p t n -> p n t"), ACT.Tanh, scale=0.0625)
+            halves = (slice(0, 2), slice(2, 4)) if c == NCH - 1 else (slice(0, 4),)
+            for ts in halves:
+                nc.scalar.activation(y32[:, ts, :], diff[:, ts, :], ACT.Tanh, scale=0.0625)
+                nc.sync.dma_start(rows[:, ts, cols], y32[:, ts, :])
+            if c == 2:
+                nc.vector.tensor_copy(y16[:], y32[:].rearrange("p t n -> p n t"))
+            nc.vector.quantize_mx(
+                out=out_w[:, cols].bitcast(FP8X4),
+                scales=out_s[:, cols],
+                in_=y16[:].rearrange("p n t -> p (n t)"),
+            )
+            nc.sync.dma_start(words_out[:, cols], out_w[:, cols].bitcast(I32))
+        for q in range(4):
+            nc.sync.dma_start(out_2[0, 4 * q : 4 * q + 4, :].bitcast(I32), out_s[32 * q : 32 * q + 4, :].bitcast(I32))

@@ -42,21 +42,22 @@ def tile_picked_candtwo_tanh_po_kernel(
         ws = sb([P, S], U8, "ws", "slot_b")
         gain = sb([P, PACK], F32, "gain")
 
-        def spread(rows, width):
-            return rows.bitcast(I32).unsqueeze(0).to_broadcast([8, 4, width // 4])
-
+        nc.vector.memset(xs[:].bitcast(I32), 0)
+        nc.vector.memset(ws[:].bitcast(I32), 0)
         nc.sync.dma_start(offs_t[:], offs)
-        for q in range(4):
-            nc.sync.dma_start(xs[32 * q : 32 * q + 32, :].bitcast(I32), spread(x_scales[0, 4 * q : 4 * q + 4, :], T))
         nc.sync.dma_start(ca_t[:], ca)
-        nc.sync.dma_start(cb_t[:], cb)
-        nc.sync.dma_start(xw[:], x_words[0].rearrange("p n t -> p (n t)").bitcast(I32))
-        nc.sync.dma_start(ww[:], w1_words[0].rearrange("p n t -> p (n t)").bitcast(I32))
         for q in range(4):
-            nc.sync.dma_start(ws[32 * q : 32 * q + 32, :].bitcast(I32), spread(w1_scales[0, 4 * q : 4 * q + 4, :], S))
+            queue = nc.sync if q % 2 == 0 else nc.scalar
+            queue.dma_start(xs[32 * q : 32 * q + 4, :].bitcast(I32), x_scales[0, 4 * q : 4 * q + 4, :].bitcast(I32))
+        nc.sync.dma_start(ww[:], w1_words[0].rearrange("p n t -> p (n t)").bitcast(I32))
+        nc.sync.dma_start(xw[:], x_words[0].rearrange("p n t -> p (n t)").bitcast(I32))
+        for q in range(4):
+            nc.sync.dma_start(ws[32 * q : 32 * q + 4, :].bitcast(I32), w1_scales[0, 4 * q : 4 * q + 4, :].bitcast(I32))
+        nc.sync.dma_start(cb_t[:], cb)
         nc.sync.dma_start(gain[:], gs.rearrange("(p t) o -> p (t o)", t=PACK))
 
-        tok_w = sb([P, S], U32, "tok_w")
+        half = 2 * CH
+        tok_w0 = sb([P, half], U32, "tok_w0")
         tok_s = sb([P, S], U8, "tok_s")
         pair_s_raw = sb([P, 2, S], U8, "pair_s_raw")
         pair_s = sb([P, 2, S], U8, "pair_s")
@@ -65,66 +66,92 @@ def tile_picked_candtwo_tanh_po_kernel(
 
         nc.vector.tensor_copy(tok_s[:], xs[:].indirect(offs_t[:]))
         nc.vector.tensor_copy(pair_s_raw[:, 0, :], xs[:].indirect(ca_t[:]))
-        nc.vector.tensor_copy(pair_s_raw[:, 1, :], xs[:].indirect(cb_t[:]))
-        nc.vector.tensor_copy(tok_w[:], xw[:].bitcast(U32).indirect(offs_t[:]))
         nc.vector.tensor_copy(
             wd_w[:].rearrange("p (t m) -> p m t", t=PACK), ww[:].rearrange("p (m t) -> p m t", t=PACK)
         )
+        nc.vector.tensor_copy(tok_w0[:], xw[:].bitcast(U32).indirect(offs_t[:, : half // 16]))
         nc.vector.tensor_copy(
             wd_s[:].rearrange("p (t m) -> p t m", t=PACK), ws[:].rearrange("p (m t) -> p t m", t=PACK)
         )
+        nc.vector.tensor_copy(pair_s_raw[:, 1, :], xs[:].indirect(cb_t[:]))
         nc.vector.tensor_copy(
             pair_s[:].rearrange("p l (t m) -> p l t m", t=PACK),
             pair_s_raw[:].rearrange("p l (m t) -> p l t m", t=PACK),
         )
-        pair_w = []
-        for lst, slot in ((ca_t, "slot_a"), (cb_t, "slot_b")):
-            picked = sb([P, S], U32, "picked_" + slot, slot)
-            nc.vector.tensor_copy(picked[:].rearrange("p (t m) -> p m t", t=PACK), xw[:].bitcast(U32).indirect(lst[:]))
-            pair_w.append(picked)
+        late = sb([P, 2 * S + half], U32, "late", "slot_b")
+        pair_w = [late[:, :S], late[:, S : 2 * S]]
+        tok_w1 = late[:, 2 * S :]
+        nc.vector.tensor_copy(pair_w[0].rearrange("p (t m) -> p m t", t=PACK), xw[:].bitcast(U32).indirect(ca_t[:]))
+        nc.vector.tensor_copy(tok_w1, xw[:].bitcast(U32).indirect(offs_t[:, half // 16 :]))
+        nc.vector.tensor_copy(pair_w[1].rearrange("p (t m) -> p m t", t=PACK), xw[:].bitcast(U32).indirect(cb_t[:]))
 
-        hid = []
-        for c in range(NCH):
-            cols = slice(c * CH, (c + 1) * CH)
-            bank = psum.tile([P, PACK, CH], F32, name="hid%d" % c)
+        def layer(out, t, words, cols):
+            m = slice(t * P, (t + 1) * P)
+            nc.tensor.matmul_mx(
+                out=out,
+                lhsT=wd_w[:, m].bitcast(FP8X4),
+                lhsT_scale=wd_s[:, m],
+                rhs=words.bitcast(FP8X4),
+                rhs_scale=tok_s[:, cols],
+                start=True,
+                stop=True,
+            )
+
+        rect = sb([P, PACK, half], F32, "rect")
+        planes = sb([P, PACK, half], BF16, "planes", "slot_z")
+        for u in range(2):
+            bank = psum.tile([P, 2, half], F32, name="hid_s%d" % u, tag="bank%d" % u)
+            for e in range(2):
+                layer(bank[:, e, :], 2 * u + e, tok_w0[:], slice(0, half))
+            nc.scalar.activation(rect[:, 2 * u : 2 * u + 2, :], bank[:], ACT.Relu)
+            for t in (2 * u, 2 * u + 1):
+                nc.scalar.activation(planes[:, t, :], rect[:, t, :], ACT.Copy, scale=gain[:, t : t + 1])
+        hid = {}
+        for c in (2, 3):
+            hid[c] = psum.tile([P, PACK, CH], F32, name="hid_v%d" % c, tag="bank%d" % c)
             for t in range(PACK):
-                m = slice(t * P, (t + 1) * P)
-                nc.tensor.matmul_mx(
-                    out=bank[:, t, :],
-                    lhsT=wd_w[:, m].bitcast(FP8X4),
-                    lhsT_scale=wd_s[:, m],
-                    rhs=tok_w[:, cols].bitcast(FP8X4),
-                    rhs_scale=tok_s[:, cols],
-                    start=True,
-                    stop=True,
-                )
-            hid.append(bank)
+                layer(hid[c][:, t, :], t, tok_w1[:, (c - 2) * CH : (c - 1) * CH], slice(c * CH, (c + 1) * CH))
 
         diffs = []
+        zs = [sb([P, 2, CH * PACK], BF16, "z%d" % c)[:] for c in range(2)]
+        for c in range(2):
+            nc.scalar.copy(
+                zs[c][:, 0, :].rearrange("p (a i t) -> p a t i", i=4, t=PACK),
+                planes[:, :, c * CH : (c + 1) * CH].rearrange("p t (a i) -> p a t i", i=4),
+            )
+        z_late = sb([P, 4, CH * PACK], BF16, "z_late", "slot_z")
+        zs = zs + [z_late[:, 0:2, :], z_late[:, 2:4, :]]
         for c in range(NCH):
-            z = sb([P, 2, CH * PACK], BF16, "z%d" % c)
+            z = zs[c]
             z_w = sb([P, 2, CH], U32, "z_w%d" % c)
             z_s = sb([P, 2, CH], U8, "z_s%d" % c)
-            nc.vector.scalar_tensor_tensor(
-                out=z[:, 0, :].rearrange("p (n t) -> p n t", t=PACK),
-                in0=hid[c][:].rearrange("p t n -> p n t"),
-                scalar=0.0,
-                in1=gain[:].unsqueeze(1).to_broadcast([P, CH, PACK]),
-                op0=ALU.max,
-                op1=ALU.mult,
-            )
+            if c >= 2:
+                nc.vector.scalar_tensor_tensor(
+                    out=z[:, 0, :].rearrange("p (n t) -> p n t", t=PACK),
+                    in0=hid[c][:].rearrange("p t n -> p n t"),
+                    scalar=0.0,
+                    in1=gain[:].unsqueeze(1).to_broadcast([P, CH, PACK]),
+                    op0=ALU.max,
+                    op1=ALU.mult,
+                )
             nc.vector.tensor_scalar(out=z[:, 1, :], in0=z[:, 0, :], scalar1=-1.0, scalar2=None, op0=ALU.mult)
             nc.vector.quantize_mx(
                 out=z_w[:].rearrange("p l n -> p (l n)").bitcast(FP8X4),
                 scales=z_s[:].rearrange("p l n -> p (l n)"),
-                in_=z[:].rearrange("p l n -> p (l n)"),
+                in_=z.rearrange("p l n -> p (l n)"),
             )
-            diff = psum.tile([P, PACK, CH], F32, name="diff%d" % c)
+            if c < NCH - 1:
+                bank = psum.tile([P, PACK, CH], F32, name="diff%d" % c)
+                diff = [bank[:, t, :] for t in range(PACK)]
+                diffs.append(bank)
+            else:
+                diff = [psum.tile([P, CH], F32, name="last%d" % t, tag="bank%d" % t)[:] for t in range(PACK)]
+                diffs.append(diff)
             for t in range(PACK):
                 m = slice(t * P, (t + 1) * P)
                 for l in range(2):
                     nc.tensor.matmul_mx(
-                        out=diff[:, t, :],
+                        out=diff[t],
                         lhsT=pair_w[l][:, m].bitcast(FP8X4),
                         lhsT_scale=pair_s[:, l, m],
                         rhs=z_w[:, l, :].bitcast(FP8X4),
@@ -132,7 +159,6 @@ def tile_picked_candtwo_tanh_po_kernel(
                         start=(l == 0),
                         stop=(l == 1),
                     )
-            diffs.append(diff)
 
         out_w = sb([P, S], U32, "out_w")
         out_s = sb([P, S], U8, "out_s")
@@ -143,19 +169,27 @@ def tile_picked_candtwo_tanh_po_kernel(
             diff = diffs[c]
             y16 = sb([P, CH, PACK], BF16, "y16_%d" % c)
             y32 = sb([P, PACK, CH], F32, "y32_%d" % c)
-            if c != 2:
+            last = c == NCH - 1
+            if last:
+                for t in range(PACK):
+                    nc.scalar.activation(y32[:, t, :], diff[t], ACT.Tanh, scale=0.0625)
+            else:
+                nc.scalar.activation(y32[:], diff[:], ACT.Tanh, scale=0.0625)
+            (nc.scalar if last else nc.sync).dma_start(rows[:, :, cols], y32[:])
+            if c == 0:
                 nc.scalar.activation(y16[:], diff[:].rearrange("p t n -> p n t"), ACT.Tanh, scale=0.0625)
-            halves = (slice(0, 2), slice(2, 4)) if c == NCH - 1 else (slice(0, 4),)
-            for ts in halves:
-                nc.scalar.activation(y32[:, ts, :], diff[:, ts, :], ACT.Tanh, scale=0.0625)
-                nc.sync.dma_start(rows[:, ts, cols], y32[:, ts, :])
-            if c == 2:
-                nc.vector.tensor_copy(y16[:], y32[:].rearrange("p t n -> p n t"))
+            if c > 0:
+                nc.vector.tensor_copy(
+                    y16[:].rearrange("p (a i) t -> p a t i", i=4), y32[:].rearrange("p t (a i) -> p a t i", i=4)
+                )
             nc.vector.quantize_mx(
                 out=out_w[:, cols].bitcast(FP8X4),
                 scales=out_s[:, cols],
                 in_=y16[:].rearrange("p n t -> p (n t)"),
             )
-            nc.sync.dma_start(words_out[:, cols], out_w[:, cols].bitcast(I32))
+            if c >= 2:
+                done = slice(0, 3 * CH) if c == 2 else cols
+                nc.sync.dma_start(words_out[:, done], out_w[:, done].bitcast(I32))
         for q in range(4):
-            nc.sync.dma_start(out_2[0, 4 * q : 4 * q + 4, :].bitcast(I32), out_s[32 * q : 32 * q + 4, :].bitcast(I32))
+            queue = nc.sync if q % 2 == 0 else nc.scalar
+            queue.dma_start(out_2[0, 4 * q : 4 * q + 4, :].bitcast(I32), out_s[32 * q : 32 * q + 4, :].bitcast(I32))

from contextlib import ExitStack

import concourse.mybir as mybir

FLOPS = 805306368

F32 = mybir.dt.float32
BF16 = mybir.dt.bfloat16
I32 = mybir.dt.int32
U32 = mybir.dt.uint32
U16 = mybir.dt.uint16
U8 = mybir.dt.uint8
FP8X4 = mybir.dt.float8_e4m3fn_x4
ALU = mybir.AluOpType
ACT = mybir.ActivationFunctionType

P = 128
PACK = 4
T = 2048
S = 512
CH = 128
NCH = S // CH


def tile_picked_candtwo_tanh_po_kernel(
    tc, x_words, x_scales, w1_words, w1_scales, gs, offs, ca, cb, out_0, out_1, out_2
):
    nc = tc.nc
    with ExitStack() as ctx:
        keep = ctx.enter_context(tc.tile_pool(name="keep", bufs=1))
        psum = ctx.enter_context(tc.psum_pool(name="psum", bufs=1))

        def sb(shape, dtype, name, tag=None):
            return keep.tile(shape, dtype, name=name, tag=tag or name, align_bytes=64)

        offs_t = keep.tile([P, S // 16], U16, name="offs_t")
        ca_t = keep.tile([P, S // 16], U16, name="ca_t")
        cb_t = keep.tile([P, S // 16], U16, name="cb_t")
        xw = sb([P, T], I32, "xw")
        xs = sb([P, T], U8, "xs")
        ww = sb([P, S], I32, "ww")
        ws = sb([P, S], U8, "ws", "slot_b")
        gain = sb([P, PACK], F32, "gain")

        nc.vector.memset(xs[:].bitcast(I32), 0)
        nc.vector.memset(ws[:].bitcast(I32), 0)
        nc.sync.dma_start(offs_t[:], offs)
        nc.sync.dma_start(ca_t[:], ca)
        for q in range(4):
            queue = nc.sync if q % 2 == 0 else nc.scalar
            queue.dma_start(xs[32 * q : 32 * q + 4, :].bitcast(I32), x_scales[0, 4 * q : 4 * q + 4, :].bitcast(I32))
        nc.sync.dma_start(ww[:], w1_words[0].rearrange("p n t -> p (n t)").bitcast(I32))
        nc.sync.dma_start(xw[:], x_words[0].rearrange("p n t -> p (n t)").bitcast(I32))
        for q in range(4):
            nc.sync.dma_start(ws[32 * q : 32 * q + 4, :].bitcast(I32), w1_scales[0, 4 * q : 4 * q + 4, :].bitcast(I32))
        nc.sync.dma_start(cb_t[:], cb)
        nc.sync.dma_start(gain[:], gs.rearrange("(p t) o -> p (t o)", t=PACK))

        half = 2 * CH
        tok_w0 = sb([P, half], U32, "tok_w0")
        tok_s = sb([P, S], U8, "tok_s")
        pair_s_raw = sb([P, 2, S], U8, "pair_s_raw")
        pair_s = sb([P, 2, S], U8, "pair_s")
        wd_w = sb([P, S], I32, "wd_w")
        wd_s = sb([P, S], U8, "wd_s")

        nc.vector.tensor_copy(tok_s[:], xs[:].indirect(offs_t[:]))
        nc.vector.tensor_copy(pair_s_raw[:, 0, :], xs[:].indirect(ca_t[:]))
        nc.vector.tensor_copy(
            wd_w[:].rearrange("p (t m) -> p m t", t=PACK), ww[:].rearrange("p (m t) -> p m t", t=PACK)
        )
        nc.vector.tensor_copy(tok_w0[:], xw[:].bitcast(U32).indirect(offs_t[:, : half // 16]))
        nc.vector.tensor_copy(
            wd_s[:].rearrange("p (t m) -> p t m", t=PACK), ws[:].rearrange("p (m t) -> p t m", t=PACK)
        )
        nc.vector.tensor_copy(pair_s_raw[:, 1, :], xs[:].indirect(cb_t[:]))
        nc.vector.tensor_copy(
            pair_s[:].rearrange("p l (t m) -> p l t m", t=PACK),
            pair_s_raw[:].rearrange("p l (m t) -> p l t m", t=PACK),
        )
        late = sb([P, 2 * S + half], U32, "late", "slot_b")
        pair_w = [late[:, :S], late[:, S : 2 * S]]
        tok_w1 = late[:, 2 * S :]
        nc.vector.tensor_copy(pair_w[0].rearrange("p (t m) -> p m t", t=PACK), xw[:].bitcast(U32).indirect(ca_t[:]))
        nc.vector.tensor_copy(tok_w1, xw[:].bitcast(U32).indirect(offs_t[:, half // 16 :]))
        nc.vector.tensor_copy(pair_w[1].rearrange("p (t m) -> p m t", t=PACK), xw[:].bitcast(U32).indirect(cb_t[:]))

        def layer(out, t, words, cols):
            m = slice(t * P, (t + 1) * P)
            nc.tensor.matmul_mx(
                out=out,
                lhsT=wd_w[:, m].bitcast(FP8X4),
                lhsT_scale=wd_s[:, m],
                rhs=words.bitcast(FP8X4),
                rhs_scale=tok_s[:, cols],
                start=True,
                stop=True,
            )

        rect = sb([P, PACK, half], F32, "rect")
        planes = sb([P, PACK, half], BF16, "planes", "slot_z")
        for u in range(2):
            bank = psum.tile([P, 2, half], F32, name="hid_s%d" % u, tag="bank%d" % u)
            for e in range(2):
                layer(bank[:, e, :], 2 * u + e, tok_w0[:], slice(0, half))
            nc.scalar.activation(rect[:, 2 * u : 2 * u + 2, :], bank[:], ACT.Relu)
            for t in (2 * u, 2 * u + 1):
                nc.scalar.activation(planes[:, t, :], rect[:, t, :], ACT.Copy, scale=gain[:, t : t + 1])
        hid = {}
        for c in (2, 3):
            hid[c] = psum.tile([P, PACK, CH], F32, name="hid_v%d" % c, tag="bank%d" % c)
            for t in range(PACK):
                layer(hid[c][:, t, :], t, tok_w1[:, (c - 2) * CH : (c - 1) * CH], slice(c * CH, (c + 1) * CH))

        diffs = []
        zs = [sb([P, 2, CH * PACK], BF16, "z%d" % c)[:] for c in range(2)]
        for c in range(2):
            nc.scalar.copy(
                zs[c][:, 0, :].rearrange("p (a i t) -> p a t i", i=4, t=PACK),
                planes[:, :, c * CH : (c + 1) * CH].rearrange("p t (a i) -> p a t i", i=4),
            )
        z_late = sb([P, 4, CH * PACK], BF16, "z_late", "slot_z")
        zs = zs + [z_late[:, 0:2, :], z_late[:, 2:4, :]]
        for c in range(NCH):
            z = zs[c]
            z_w = sb([P, 2, CH], U32, "z_w%d" % c)
            z_s = sb([P, 2, CH], U8, "z_s%d" % c)
            if c >= 2:
                nc.vector.scalar_tensor_tensor(
                    out=z[:, 0, :].rearrange("p (n t) -> p n t", t=PACK),
                    in0=hid[c][:].rearrange("p t n -> p n t"),
                    scalar=0.0,
                    in1=gain[:].unsqueeze(1).to_broadcast([P, CH, PACK]),
                    op0=ALU.max,
                    op1=ALU.mult,
                )
            nc.vector.tensor_scalar(out=z[:, 1, :], in0=z[:, 0, :], scalar1=-1.0, scalar2=None, op0=ALU.mult)
            nc.vector.quantize_mx(
                out=z_w[:].rearrange("p l n -> p (l n)").bitcast(FP8X4),
                scales=z_s[:].rearrange("p l n -> p (l n)"),
                in_=z.rearrange("p l n -> p (l n)"),
            )
            if c < NCH - 1:
                bank = psum.tile([P, PACK, CH], F32, name="diff%d" % c)
                diff = [bank[:, t, :] for t in range(PACK)]
                diffs.append(bank)
            else:
                diff = [psum.tile([P, CH], F32, name="last%d" % t, tag="bank%d" % t)[:] for t in range(PACK)]
                diffs.append(diff)
            for t in range(PACK):
                m = slice(t * P, (t + 1) * P)
                for l in range(2):
                    nc.tensor.matmul_mx(
                        out=diff[t],
                        lhsT=pair_w[l][:, m].bitcast(FP8X4),
                        lhsT_scale=pair_s[:, l, m],
                        rhs=z_w[:, l, :].bitcast(FP8X4),
                        rhs_scale=z_s[:, l, :],
                        start=(l == 0),
                        stop=(l == 1),
                    )

        out_w = sb([P, S], U32, "out_w")
        out_s = sb([P, S], U8, "out_s")
        rows = out_0.rearrange("(p t) n -> p t n", t=PACK)
        words_out = out_1[0].rearrange("p n t -> p (n t)").bitcast(I32)
        for c in range(NCH):
            cols = slice(c * CH, (c + 1) * CH)
            diff = diffs[c]
            y16 = sb([P, CH, PACK], BF16, "y16_%d" % c)
            y32 = sb([P, PACK, CH], F32, "y32_%d" % c)
            last = c == NCH - 1
            if last:
                for t in range(PACK):
                    nc.scalar.activation(y32[:, t, :], diff[t], ACT.Tanh, scale=0.0625)
            else:
                nc.scalar.activation(y32[:], diff[:], ACT.Tanh, scale=0.0625)
            (nc.scalar if last else nc.sync).dma_start(rows[:, :, cols], y32[:])
            if c == 0:
                nc.scalar.activation(y16[:], diff[:].rearrange("p t n -> p n t"), ACT.Tanh, scale=0.0625)
            if c > 0:
                nc.vector.tensor_copy(
                    y16[:].rearrange("p (a i) t -> p a t i", i=4), y32[:].rearrange("p t (a i) -> p a t i", i=4)
                )
            nc.vector.quantize_mx(
                out=out_w[:, cols].bitcast(FP8X4),
                scales=out_s[:, cols],
                in_=y16[:].rearrange("p n t -> p (n t)"),
            )
            if c >= 2:
                done = slice(0, 3 * CH) if c == 2 else cols
                nc.sync.dma_start(words_out[:, done], out_w[:, done].bitcast(I32))
        for q in range(4):
            queue = nc.sync if q % 2 == 0 else nc.scalar
            queue.dma_start(out_2[0, 4 * q : 4 * q + 4, :].bitcast(I32), out_s[32 * q : 32 * q + 4, :].bitcast(I32))
